import numpy as np
import ml_dtypes


def mxq(x, axis, fmt="e4m3"):
    dtype, down = {"e4m3": (ml_dtypes.float8_e4m3fn, 7), "e5m2": (ml_dtypes.float8_e5m2, 14)}[fmt]
    v = np.moveaxis(np.asarray(x, np.float32).astype(ml_dtypes.bfloat16).astype(np.float64), axis, -1)
    blocks = v.reshape(v.shape[:-1] + (-1, 32))
    amax = np.abs(blocks).max(-1, keepdims=True)
    byte = np.maximum(np.where(amax > 0, np.frexp(amax)[1] - 1 + 127, 0) - down, 1)
    scale = np.exp2(byte - 127.0)
    codes = (blocks / scale).astype(np.float32).astype(dtype).astype(np.float64)
    return np.moveaxis((codes * scale).reshape(v.shape), -1, axis)


WIDE = False


def mx_kscale(k):
    if not WIDE:
        return np.ones(k)
    levels = np.array([10, -10, 5, -5, 0])
    if k % 512:
        return np.exp2(np.random.permutation(np.resize(levels, k // 32))).repeat(32)
    a = np.empty((k // 512, 16))
    for p in range(k // 512):
        a[p, :8] = np.random.permutation(np.resize(levels, 8))
        for g in range(8):
            far = levels[np.abs(levels - a[p, g]) >= 10]
            a[p, g + 8] = far[np.random.randint(len(far))]
    return np.exp2(a.ravel()).repeat(32)


def f64(x):
    return np.asarray(x).astype(np.float64)


def striped(idx):
    return np.tile(np.asarray(idx).reshape(-1, 16).T, (8, 1)).astype(np.uint16)


def unstriped(offs):
    return offs[:16].T.reshape(-1).astype(np.int64)


E2M1 = np.array([0.0, 0.5, 1.0, 1.5, 2.0, 3.0, 4.0, 6.0, -0.0, -0.5, -1.0, -1.5, -2.0, -3.0, -4.0, -6.0])


def pack_weight(w, fmt):
    k, n = w.shape
    w = f64(np.asarray(w, np.float32).astype(ml_dtypes.bfloat16)).reshape(k // 32, 32, n)
    amax = np.abs(w).max(1)
    if fmt == "e4m3":
        byte = np.frexp(amax)[1] - 1 + 127 - 7
    else:
        mant, ex = np.frexp(amax / 6.0)
        byte = np.where(mant > 0.5, ex, ex - 1) + 127
    byte = np.clip(np.where(amax > 0, byte, 1), 1, 254)
    scaled = (w * np.exp2(127.0 - byte)[:, None, :]).reshape(k, n).astype(np.float32)
    by_word = np.ascontiguousarray(scaled.reshape(k // 512, 128, 4, n).transpose(0, 1, 3, 2))
    if fmt == "e4m3":
        words = by_word.astype(ml_dtypes.float8_e4m3fn).view(np.uint8)
    else:
        c = by_word.astype(ml_dtypes.float4_e2m1fn).view(np.uint8) & 0xF
        words = (c[..., 0::2] | (c[..., 1::2] << 4)).reshape(k // 512, 128, 2 * n)
    return np.ascontiguousarray(words), np.ascontiguousarray(byte.astype(np.uint8).reshape(k // 512, 16, n))


def unpack_weight(words, scales, fmt):
    g, _, n = scales.shape
    words = np.ascontiguousarray(words).reshape(g, 128, n, -1)
    if fmt == "e4m3":
        vals = words.view(ml_dtypes.float8_e4m3fn).astype(np.float64)
    else:
        nib = np.empty((g, 128, n, 4), np.uint8)
        nib[..., 0::2] = words & 0xF
        nib[..., 1::2] = words >> 4
        vals = E2M1[nib]
    vals = vals * np.repeat(np.exp2(scales.astype(np.float64) - 127.0), 8, axis=1)[..., None]
    return vals.transpose(0, 1, 3, 2).reshape(g * 512, n)


def sigmoid(v):
    return 1.0 / (1.0 + np.exp(-v))


D, E, T, I, Q, G = 512, 512, 2048, 512, 128, 32


def setup_inputs():
    n = np.random.standard_normal
    idx = np.random.permutation(T)[:I]
    fd = mx_kscale(D)
    fe = mx_kscale(E)
    keysp = pack_weight(n((D, T)) / fd[:, None], "e4m3")
    valsp = pack_weight(n((E, T)) / fe[:, None], "e4m3")
    return {
        "query": (n((D, Q)) * 0.8 / np.sqrt(D) * fd[:, None]).astype(np.float32),
        "keys_words": keysp[0],
        "keys_scales": keysp[1],
        "th": (np.random.uniform(-0.5, 0.5, (Q, 1))).astype(np.float32),
        "sharp": (np.random.uniform(1.0, 3.0, (Q, 1))).astype(np.float32),
        "gout": (n((E, Q)) * 1 / np.sqrt(E) * fe[:, None]).astype(np.float32),
        "vals_words": valsp[0],
        "vals_scales": valsp[1],
        "base": (0.5 * n((Q, I))).astype(np.float32),
        "offs": striped(idx),
    }


def reference(query, keys_words, keys_scales, th, sharp, gout, vals_words, vals_scales, base, offs):
    idx = unstriped(offs)
    keysu = unpack_weight(keys_words, keys_scales, "e4m3")
    valsu = unpack_weight(vals_words, vals_scales, "e4m3")
    queryq = mxq(f64(query), 0, "e4m3")
    keysidxg = keysu[:, idx]
    a = queryq.T @ keysidxg
    s = a.reshape(Q, G, I // G).mean(axis=2) * f64(sharp)
    p = np.exp(s - np.max(s, axis=1, keepdims=True))
    z = np.sum(p, axis=1, keepdims=True)
    r = p / z
    rr = np.repeat(r, I // G, axis=1)
    goutq = mxq(f64(gout), 0, "e4m3")
    valsidxg = valsu[:, idx]
    c0 = goutq.T @ valsidxg
    drr = c0 * sigmoid(a - f64(th))
    dr = drr.reshape(Q, G, I // G).sum(axis=2)
    dz = np.sum(dr * p / np.square(z) * (-1.0), axis=1, keepdims=True)
    dp = dr / z + dz
    ds = dp * p
    e1 = ds * f64(sharp) / 16.0
    r1 = np.repeat(e1, I // G, axis=1)
    da = c0 * rr * sigmoid(a - f64(th)) * (1.0 - sigmoid(a - f64(th))) + r1
    hda = da * 32.0 * 2.0 * 32.0
    he1 = hda.reshape(Q, G, I // G).sum(axis=2)
    hds = he1 / 16.0 * f64(sharp)
    hdp = hds * p
    hdz = np.sum(hdp, axis=1, keepdims=True)
    hdr = hdp / z + hdz * (-1.0) / np.square(z) * p
    r51 = np.repeat(hdr, I // G, axis=1)
    hrr = hda * (1.0 - sigmoid(a - f64(th))) * sigmoid(a - f64(th)) * c0
    hr = hrr.reshape(Q, G, I // G).sum(axis=2)
    hz = np.sum(hdp * dr / np.square(z) * (-1.0), axis=1, keepdims=True) + np.sum(hdz * (-1.0) * dr * p / np.square(np.square(z)) * (-1.0), axis=1, keepdims=True) * z * 2.0 + np.sum(hr * p / np.square(z) * (-1.0), axis=1, keepdims=True)
    hp = hds * dp + hdz * (-1.0) / np.square(z) * dr + hr / z + hz
    hs = hp * p
    e52 = hs * f64(sharp) / 16.0
    r52 = np.repeat(e52, I // G, axis=1)
    ha = hda * (1.0 - sigmoid(a - f64(th))) * c0 * rr * sigmoid(a - f64(th)) * (1.0 - sigmoid(a - f64(th))) + hda * c0 * rr * sigmoid(a - f64(th)) * (-1.0) * sigmoid(a - f64(th)) * (1.0 - sigmoid(a - f64(th))) + r51 * c0 * sigmoid(a - f64(th)) * (1.0 - sigmoid(a - f64(th))) + r52
    y = ha + f64(base)
    return y

@@ -1,0 +1,197 @@
+from contextlib import ExitStack
+
+import concourse.mybir as mybir
+
+D, E, T, I, Q, G = 512, 512, 2048, 512, 128, 32
+FLOPS = 2 * D * Q * I + 2 * E * Q * I
+
+F32 = mybir.dt.float32
+BF16 = mybir.dt.bfloat16
+I32 = mybir.dt.int32
+U32 = mybir.dt.uint32
+U16 = mybir.dt.uint16
+U8 = mybir.dt.uint8
+FP8X4 = mybir.dt.float8_e4m3fn_x4
+ALU = mybir.AluOpType
+ACT = mybir.ActivationFunctionType
+AXIS_X = mybir.AxisListType.X
+
+P = 128
+PACK = 4
+PAGE = I // G
+HALF = I // 2
+PENALTY = 32.0 * 2.0 * 32.0
+
+
+def tile_attend_gppagetimessigmoid_kernel(tc, query, keys_words, keys_scales, th, sharp, gout,
+                                           vals_words, vals_scales, base, offs, out):
+    nc = tc.nc
+    mult, add, sub = ALU.mult, ALU.add, ALU.subtract
+
+    with ExitStack() as ctx:
+        sb = ctx.enter_context(tc.tile_pool(name="sb", bufs=1))
+        ps = ctx.enter_context(tc.psum_pool(name="ps", bufs=1))
+
+        def tile(name, shape, dtype=F32, tag=None):
+            return sb.tile(shape, dtype, name=name, tag=tag or name, align_bytes=64)
+
+        def pages(ap):
+            return ap.rearrange("p (g j) -> p g j", j=PAGE)
+
+        def spread(ap):
+            return ap.unsqueeze(2).to_broadcast([P, ap.shape[1], PAGE])
+
+        def load_words(name, words, tag=None):
+            pool_words = tile(name, [P, T], I32, tag)
+            nc.sync.dma_start(pool_words[:], words[0].rearrange("p t r -> p (t r)").bitcast(I32))
+            return pool_words
+
+        def load_scales(name, scales, zero_engine, queue):
+            plane = tile(name, [P, T], U8)
+            zero_engine.memset(plane[:].bitcast(I32), 0)
+            for quad in range(4):
+                queue.dma_start(plane[32 * quad : 32 * quad + 4, :].bitcast(I32),
+                                scales[0, 4 * quad : 4 * quad + 4, :].bitcast(I32))
+            return plane
+
+        def load_rows(name, rows):
+            raw = tile(name, [P, PACK, Q])
+            nc.sync.dma_start(raw[:], rows.rearrange("(p r) q -> p r q", r=PACK))
+            return raw
+
+        def quantise(name, raw):
+            woven = tile(name + "_woven", [P, Q, PACK], BF16)
+            nc.scalar.copy(woven[:], raw[:].rearrange("p r q -> p q r"))
+            codes = tile(name + "_codes", [P, Q], U32)
+            plane = tile(name + "_plane", [P, Q], U8)
+            nc.vector.quantize_mx(out=codes[:].bitcast(FP8X4), scales=plane[:],
+                                  in_=woven[:].rearrange("p q r -> p (q r)"))
+            return codes, plane
+
+        offsets = sb.tile([P, I // 16], U16, name="offsets")
+        nc.sync.dma_start(offsets[:], offs)
+        sharp_col = tile("sharp_col", [P, 1])
+        nc.sync.dma_start(sharp_col[:], sharp)
+        th_col = tile("th_col", [P, 1])
+        nc.sync.dma_start(th_col[:], th)
+        keys_plane = load_scales("keys_plane", keys_scales, nc.vector, nc.sync)
+        keys_pool = load_words("keys_pool", keys_words)
+        query_raw = load_rows("query_raw", query)
+        gout_raw = load_rows("gout_raw", gout)
+        vals_plane = load_scales("vals_plane", vals_scales, nc.gpsimd, nc.sync)
+        vals_pool = load_words("vals_pool", vals_words)
+        base_sb = tile("base_sb", [P, I])
+        nc.sync.dma_start(base_sb[:], base)
+        query_codes, query_plane = quantise("query", query_raw)
+
+        keys_bytes = tile("keys_bytes", [P, I], U8)
+        nc.vector.tensor_copy(keys_bytes[:], keys_plane[:].indirect(offsets[:]))
+        keys_codes = tile("keys_codes", [P, I], U32)
+        nc.vector.tensor_copy(keys_codes[:], keys_pool[:].bitcast(U32).indirect(offsets[:]))
+        score = ps.tile([P, I], F32, name="score")
+        nc.tensor.matmul_mx(out=score[:], lhsT=query_codes[:].bitcast(FP8X4), lhsT_scale=query_plane[:],
+                            rhs=keys_codes[:].bitcast(FP8X4), rhs_scale=keys_bytes[:], start=True, stop=True)
+
+        gout_codes, gout_plane = quantise("gout", gout_raw)
+        vals_bytes = tile("vals_bytes", [P, I], U8)
+        nc.vector.tensor_copy(vals_bytes[:], vals_plane[:].indirect(offsets[:]))
+
+        vals_codes = tile("vals_codes", [P, I], U32)
+        drr2 = tile("drr2", [P, I])
+        w = tile("w", [P, I])
+        c0 = []
+        for h in range(2):
+            cols = slice(h * HALF, (h + 1) * HALF)
+            nc.vector.tensor_copy(vals_codes[:, cols],
+                                  vals_pool[:].bitcast(U32).indirect(offsets[:, h * HALF // 16 : (h + 1) * HALF // 16]))
+            bank = ps.tile([P, HALF], F32, name="c0_%d" % h)
+            nc.tensor.matmul_mx(out=bank[:], lhsT=gout_codes[:].bitcast(FP8X4), lhsT_scale=gout_plane[:],
+                                rhs=vals_codes[:, cols].bitcast(FP8X4), rhs_scale=vals_bytes[:, cols],
+                                start=True, stop=True)
+            c0.append(bank)
+
+        def column(name, source, factor):
+            col = tile(name, [P, 1])
+            nc.scalar.mul(col[:], source[:], factor)
+            return col
+
+        th_bias = column("th_bias", th_col, -0.5)
+        neg_k = column("neg_k", sharp_col, -1.0 / PAGE)
+        neg_half_k = column("neg_half_k", sharp_col, -0.5 / PAGE)
+        pen_k = column("pen_k", sharp_col, PENALTY / PAGE)
+        neg_pen_k = column("neg_pen_k", sharp_col, -PENALTY / PAGE)
+
+        gate = tile("gate", [P, I])
+        nc.scalar.activation(gate[:], score[:], ACT.Tanh, bias=th_bias[:], scale=0.5)
+        gate_sq = tile("gate_sq", [P, I])
+        nc.scalar.activation(gate_sq[:], gate[:], ACT.Square)
+
+        score_sum = tile("score_sum", [P, G])
+        nc.vector.tensor_reduce(score_sum[:], pages(score[:]), AXIS_X, add)
+        neg_s = tile("neg_s", [P, G])
+        neg_top = tile("neg_top", [P, 1])
+        nc.vector.tensor_scalar(neg_s[:], score_sum[:], neg_k[:], None, mult, ALU.min, accum_out=neg_top[:])
+        p = tile("p", [P, G])
+        z = tile("z", [P, 1])
+        nc.scalar.activation(p[:], neg_s[:], ACT.Exp, bias=neg_top[:], scale=-1.0, accum_out=z[:])
+        z_inv = tile("z_inv", [P, 1])
+        nc.vector.reciprocal(z_inv[:], z[:])
+        r = tile("r", [P, G])
+        nc.vector.tensor_scalar(r[:], p[:], z_inv[:], None, mult)
+        neg_quarter_r = tile("neg_quarter_r", [P, G])
+        nc.vector.tensor_scalar(neg_quarter_r[:], p[:], z_inv[:], -0.25, mult, mult)
+        slope = tile("slope", [P, I])
+        nc.vector.scalar_tensor_tensor(pages(slope[:]), pages(gate_sq[:]), 1.0, spread(neg_quarter_r[:]), sub, mult)
+
+        for h in range(2):
+            cols = slice(h * HALF, (h + 1) * HALF)
+            nc.vector.scalar_tensor_tensor(drr2[:, cols], gate[:, cols], 1.0, c0[h][:], add, mult)
+        for h in range(2):
+            cols = slice(h * HALF, (h + 1) * HALF)
+            nc.vector.tensor_tensor(w[:, cols], c0[h][:], slope[:, cols], mult)
+        w_sq = tile("w_sq", [P, I])
+        nc.scalar.activation(w_sq[:], w[:], ACT.Square)
+
+        dr2 = tile("dr2", [P, G])
+        nc.vector.tensor_reduce(dr2[:], pages(drr2[:]), AXIS_X, add)
+        w_sum = tile("w_sum", [P, G])
+        nc.vector.tensor_reduce(w_sum[:], pages(w[:]), AXIS_X, add)
+        neg_krd = tile("neg_krd", [P, G])
+        neg_km = tile("neg_km", [P, 1])
+        nc.vector.scalar_tensor_tensor(neg_krd[:], dr2[:], neg_half_k[:], r[:], mult, mult, accum_out=neg_km[:])
+        w_sq_sum = tile("w_sq_sum", [P, G])
+        nc.vector.tensor_reduce(w_sq_sum[:], pages(w_sq[:]), AXIS_X, add)
+        e1 = tile("e1", [P, G])
+        nc.vector.scalar_tensor_tensor(e1[:], r[:], neg_km[:], neg_krd[:], mult, sub)
+        da_sum = tile("da_sum", [P, G])
+        nc.vector.scalar_tensor_tensor(da_sum[:], e1[:], float(PAGE), w_sum[:], mult, add)
+        da = tile("da", [P, I])
+        nc.vector.tensor_tensor(pages(da[:]), pages(w[:]), spread(e1[:]), add)
+        r_hds = tile("r_hds", [P, G])
+        hds_mean = tile("hds_mean", [P, 1])
+        nc.vector.scalar_tensor_tensor(r_hds[:], da_sum[:], pen_k[:], r[:], mult, mult, accum_out=hds_mean[:])
+        bend = tile("bend", [P, I])
+        nc.vector.scalar_tensor_tensor(bend[:], da[:], -PENALTY, gate[:], mult, mult)
+        hds_c = tile("hds_c", [P, G])
+        nc.vector.tensor_scalar(hds_c[:], da_sum[:], pen_k[:], hds_mean[:], mult, sub)
+        neg_j = tile("neg_j", [P, G])
+        nc.vector.scalar_tensor_tensor(neg_j[:], w_sum[:], neg_pen_k[:], hds_c[:], mult, sub)
+        factor = tile("factor", [P, I])
+        nc.vector.tensor_tensor(pages(factor[:]), pages(bend[:]), spread(hds_c[:]), add)
+        neg_l = tile("neg_l", [P, G])
+        nc.vector.tensor_tensor(neg_l[:], neg_j[:], e1[:], mult)
+        slot_term = tile("slot_term", [P, I])
+        nc.vector.tensor_tensor(slot_term[:], factor[:], w[:], mult)
+        neg_tau = tile("neg_tau", [P, G])
+        neg_tau_sum = tile("neg_tau_sum", [P, 1])
+        nc.vector.scalar_tensor_tensor(neg_tau[:], w_sq_sum[:], neg_pen_k[:], neg_l[:], mult, add, accum_out=neg_tau_sum[:])
+        based = tile("based", [P, I])
+        nc.vector.tensor_tensor(based[:], slot_term[:], base_sb[:], add)
+        e52 = tile("e52", [P, G])
+        nc.vector.scalar_tensor_tensor(e52[:], r[:], neg_tau_sum[:], neg_tau[:], mult, sub)
+        result = tile("result", [P, I])
+        for h in range(2):
+            cols = slice(h * HALF, (h + 1) * HALF)
+            nc.vector.tensor_tensor(pages(result[:, cols]), pages(based[:, cols]),
+                                    spread(e52[:, h * G // 2 : (h + 1) * G // 2]), add)
+            nc.sync.dma_start(out[:, cols], result[:, cols])

@@ -77,8 +77,8 @@ def tile_attend_gppagetimessigmoid_kernel(tc, query, keys_words, keys_scales, th
         keys_plane = load_scales("keys_plane", keys_scales, nc.vector, nc.sync)
         keys_pool = load_words("keys_pool", keys_words)
         query_raw = load_rows("query_raw", query)
+        vals_plane = load_scales("vals_plane", vals_scales, nc.vector, nc.sync)
         gout_raw = load_rows("gout_raw", gout)
-        vals_plane = load_scales("vals_plane", vals_scales, nc.gpsimd, nc.sync)
         vals_pool = load_words("vals_pool", vals_words)
         base_sb = tile("base_sb", [P, I])
         nc.sync.dma_start(base_sb[:], base)
@@ -96,19 +96,22 @@ def tile_attend_gppagetimessigmoid_kernel(tc, query, keys_words, keys_scales, th
         vals_bytes = tile("vals_bytes", [P, I], U8)
         nc.vector.tensor_copy(vals_bytes[:], vals_plane[:].indirect(offsets[:]))
 
-        vals_codes = tile("vals_codes", [P, I], U32)
         drr2 = tile("drr2", [P, I])
         w = tile("w", [P, I])
         c0 = []
-        for h in range(2):
+
+        def value_product(h, tag):
             cols = slice(h * HALF, (h + 1) * HALF)
-            nc.vector.tensor_copy(vals_codes[:, cols],
+            vals_codes = tile("vals_codes%d" % h, [P, HALF], U32, tag)
+            nc.vector.tensor_copy(vals_codes[:],
                                   vals_pool[:].bitcast(U32).indirect(offsets[:, h * HALF // 16 : (h + 1) * HALF // 16]))
             bank = ps.tile([P, HALF], F32, name="c0_%d" % h)
             nc.tensor.matmul_mx(out=bank[:], lhsT=gout_codes[:].bitcast(FP8X4), lhsT_scale=gout_plane[:],
-                                rhs=vals_codes[:, cols].bitcast(FP8X4), rhs_scale=vals_bytes[:, cols],
+                                rhs=vals_codes[:].bitcast(FP8X4), rhs_scale=vals_bytes[:, cols],
                                 start=True, stop=True)
             c0.append(bank)
+
+        value_product(0, None)
 
         def column(name, source, factor):
             col = tile(name, [P, 1])
@@ -121,12 +124,12 @@ def tile_attend_gppagetimessigmoid_kernel(tc, query, keys_words, keys_scales, th
         pen_k = column("pen_k", sharp_col, PENALTY / PAGE)
         neg_pen_k = column("neg_pen_k", sharp_col, -PENALTY / PAGE)
 
-        gate = tile("gate", [P, I])
+        gate = tile("gate", [P, I], F32, "gout_raw")
         nc.scalar.activation(gate[:], score[:], ACT.Tanh, bias=th_bias[:], scale=0.5)
         gate_sq = tile("gate_sq", [P, I])
         nc.scalar.activation(gate_sq[:], gate[:], ACT.Square)
 
-        score_sum = tile("score_sum", [P, G])
+        score_sum = tile("score_sum", [P, G], F32, "vals_plane")
         nc.vector.tensor_reduce(score_sum[:], pages(score[:]), AXIS_X, add)
         neg_s = tile("neg_s", [P, G])
         neg_top = tile("neg_top", [P, 1])
@@ -138,17 +141,20 @@ def tile_attend_gppagetimessigmoid_kernel(tc, query, keys_words, keys_scales, th
         nc.vector.reciprocal(z_inv[:], z[:])
         r = tile("r", [P, G])
         nc.vector.tensor_scalar(r[:], p[:], z_inv[:], None, mult)
-        neg_quarter_r = tile("neg_quarter_r", [P, G])
-        nc.vector.tensor_scalar(neg_quarter_r[:], p[:], z_inv[:], -0.25, mult, mult)
+        neg_r = tile("neg_r", [P, G])
+        nc.vector.tensor_scalar(neg_r[:], p[:], z_inv[:], -1.0, mult, mult)
+        value_product(1, "p")
         slope = tile("slope", [P, I])
-        nc.vector.scalar_tensor_tensor(pages(slope[:]), pages(gate_sq[:]), 1.0, spread(neg_quarter_r[:]), sub, mult)
+        for g in range(G):
+            cols = slice(g * PAGE, (g + 1) * PAGE)
+            nc.scalar.activation(slope[:, cols], gate_sq[:, cols], ACT.Identity, bias=neg_r[:, g : g + 1], scale=r[:, g : g + 1])
 
         for h in range(2):
             cols = slice(h * HALF, (h + 1) * HALF)
             nc.vector.scalar_tensor_tensor(drr2[:, cols], gate[:, cols], 1.0, c0[h][:], add, mult)
         for h in range(2):
             cols = slice(h * HALF, (h + 1) * HALF)
-            nc.vector.tensor_tensor(w[:, cols], c0[h][:], slope[:, cols], mult)
+            nc.vector.scalar_tensor_tensor(w[:, cols], c0[h][:], -0.25, slope[:, cols], mult, mult)
         w_sq = tile("w_sq", [P, I])
         nc.scalar.activation(w_sq[:], w[:], ACT.Square)
 
@@ -166,32 +172,39 @@ def tile_attend_gppagetimessigmoid_kernel(tc, query, keys_words, keys_scales, th
         da_sum = tile("da_sum", [P, G])
         nc.vector.scalar_tensor_tensor(da_sum[:], e1[:], float(PAGE), w_sum[:], mult, add)
         da = tile("da", [P, I])
-        nc.vector.tensor_tensor(pages(da[:]), pages(w[:]), spread(e1[:]), add)
+        for g in range(G):
+            cols = slice(g * PAGE, (g + 1) * PAGE)
+            nc.scalar.activation(da[:, cols], w[:, cols], ACT.Identity, bias=e1[:, g : g + 1])
         r_hds = tile("r_hds", [P, G])
         hds_mean = tile("hds_mean", [P, 1])
         nc.vector.scalar_tensor_tensor(r_hds[:], da_sum[:], pen_k[:], r[:], mult, mult, accum_out=hds_mean[:])
-        bend = tile("bend", [P, I])
-        nc.vector.scalar_tensor_tensor(bend[:], da[:], -PENALTY, gate[:], mult, mult)
         hds_c = tile("hds_c", [P, G])
         nc.vector.tensor_scalar(hds_c[:], da_sum[:], pen_k[:], hds_mean[:], mult, sub)
         neg_j = tile("neg_j", [P, G])
         nc.vector.scalar_tensor_tensor(neg_j[:], w_sum[:], neg_pen_k[:], hds_c[:], mult, sub)
-        factor = tile("factor", [P, I])
-        nc.vector.tensor_tensor(pages(factor[:]), pages(bend[:]), spread(hds_c[:]), add)
         neg_l = tile("neg_l", [P, G])
         nc.vector.tensor_tensor(neg_l[:], neg_j[:], e1[:], mult)
-        slot_term = tile("slot_term", [P, I])
-        nc.vector.tensor_tensor(slot_term[:], factor[:], w[:], mult)
         neg_tau = tile("neg_tau", [P, G])
         neg_tau_sum = tile("neg_tau_sum", [P, 1])
         nc.vector.scalar_tensor_tensor(neg_tau[:], w_sq_sum[:], neg_pen_k[:], neg_l[:], mult, add, accum_out=neg_tau_sum[:])
-        based = tile("based", [P, I])
-        nc.vector.tensor_tensor(based[:], slot_term[:], base_sb[:], add)
         e52 = tile("e52", [P, G])
         nc.vector.scalar_tensor_tensor(e52[:], r[:], neg_tau_sum[:], neg_tau[:], mult, sub)
+        based = tile("based", [P, I])
+        for g in range(G):
+            cols = slice(g * PAGE, (g + 1) * PAGE)
+            nc.scalar.activation(based[:, cols], base_sb[:, cols], ACT.Identity, bias=e52[:, g : g + 1])
+        bend = tile("bend", [P, I])
+        factor = tile("factor", [P, I])
+        slot_term = tile("slot_term", [P, I])
         result = tile("result", [P, I])
-        for h in range(2):
-            cols = slice(h * HALF, (h + 1) * HALF)
-            nc.vector.tensor_tensor(pages(result[:, cols]), pages(based[:, cols]),
-                                    spread(e52[:, h * G // 2 : (h + 1) * G // 2]), add)
+        halves = [slice(h * HALF, (h + 1) * HALF) for h in range(2)]
+        for cols in halves:
+            nc.vector.scalar_tensor_tensor(bend[:, cols], da[:, cols], -PENALTY, gate[:, cols], mult, mult)
+        for h, cols in enumerate(halves):
+            nc.vector.tensor_tensor(pages(factor[:, cols]), pages(bend[:, cols]),
+                                    spread(hds_c[:, h * G // 2 : (h + 1) * G // 2]), add)
+        for cols in halves:
+            nc.vector.tensor_tensor(slot_term[:, cols], factor[:, cols], w[:, cols], mult)
+        for cols in halves:
+            nc.vector.tensor_tensor(result[:, cols], slot_term[:, cols], based[:, cols], add)
             nc.sync.dma_start(out[:, cols], result[:, cols])

@@ -70,13 +70,13 @@ def tile_attend_gppagetimessigmoid_kernel(tc, query, keys_words, keys_scales, th
 
         offsets = sb.tile([P, I // 16], U16, name="offsets")
         nc.sync.dma_start(offsets[:], offs)
+        query_raw = load_rows("query_raw", query)
         sharp_col = tile("sharp_col", [P, 1])
         nc.sync.dma_start(sharp_col[:], sharp)
-        th_col = tile("th_col", [P, 1])
-        nc.sync.dma_start(th_col[:], th)
         keys_plane = load_scales("keys_plane", keys_scales, nc.vector, nc.sync)
         keys_pool = load_words("keys_pool", keys_words)
-        query_raw = load_rows("query_raw", query)
+        th_col = tile("th_col", [P, 1])
+        nc.sync.dma_start(th_col[:], th)
         vals_plane = load_scales("vals_plane", vals_scales, nc.vector, nc.sync)
         gout_raw = load_rows("gout_raw", gout)
         vals_pool = load_words("vals_pool", vals_words)
@@ -84,34 +84,31 @@ def tile_attend_gppagetimessigmoid_kernel(tc, query, keys_words, keys_scales, th
         nc.sync.dma_start(base_sb[:], base)
         query_codes, query_plane = quantise("query", query_raw)
 
+        halves = [slice(h * HALF, (h + 1) * HALF) for h in range(2)]
+        half_pages = [slice(h * G // 2, (h + 1) * G // 2) for h in range(2)]
+        half_list = [offsets[:, h * HALF // 16 : (h + 1) * HALF // 16] for h in range(2)]
+
+        def page_cols(g):
+            return slice(g * PAGE, (g + 1) * PAGE)
+
+        def product(name, h, pool_words, picked_bytes, codes, plane, tag=None):
+            picked = tile("%s_codes%d" % (name, h), [P, HALF], U32, tag)
+            nc.vector.tensor_copy(picked[:], pool_words[:].bitcast(U32).indirect(half_list[h]))
+            bank = ps.tile([P, HALF], F32, name="%s_bank%d" % (name, h))
+            nc.tensor.matmul_mx(out=bank[:], lhsT=codes[:].bitcast(FP8X4), lhsT_scale=plane[:],
+                                rhs=picked[:].bitcast(FP8X4), rhs_scale=picked_bytes[:, halves[h]],
+                                start=True, stop=True)
+            return bank
+
         keys_bytes = tile("keys_bytes", [P, I], U8)
         nc.vector.tensor_copy(keys_bytes[:], keys_plane[:].indirect(offsets[:]))
-        keys_codes = tile("keys_codes", [P, I], U32)
-        nc.vector.tensor_copy(keys_codes[:], keys_pool[:].bitcast(U32).indirect(offsets[:]))
-        score = ps.tile([P, I], F32, name="score")
-        nc.tensor.matmul_mx(out=score[:], lhsT=query_codes[:].bitcast(FP8X4), lhsT_scale=query_plane[:],
-                            rhs=keys_codes[:].bitcast(FP8X4), rhs_scale=keys_bytes[:], start=True, stop=True)
+        score = [product("keys", 0, keys_pool, keys_bytes, query_codes, query_plane, "keys_plane"),
+                 product("keys", 1, keys_pool, keys_bytes, query_codes, query_plane)]
 
         gout_codes, gout_plane = quantise("gout", gout_raw)
         vals_bytes = tile("vals_bytes", [P, I], U8)
         nc.vector.tensor_copy(vals_bytes[:], vals_plane[:].indirect(offsets[:]))
-
-        drr2 = tile("drr2", [P, I])
-        w = tile("w", [P, I])
-        c0 = []
-
-        def value_product(h, tag):
-            cols = slice(h * HALF, (h + 1) * HALF)
-            vals_codes = tile("vals_codes%d" % h, [P, HALF], U32, tag)
-            nc.vector.tensor_copy(vals_codes[:],
-                                  vals_pool[:].bitcast(U32).indirect(offsets[:, h * HALF // 16 : (h + 1) * HALF // 16]))
-            bank = ps.tile([P, HALF], F32, name="c0_%d" % h)
-            nc.tensor.matmul_mx(out=bank[:], lhsT=gout_codes[:].bitcast(FP8X4), lhsT_scale=gout_plane[:],
-                                rhs=vals_codes[:].bitcast(FP8X4), rhs_scale=vals_bytes[:, cols],
-                                start=True, stop=True)
-            c0.append(bank)
-
-        value_product(0, None)
+        c0 = [product("vals", h, vals_pool, vals_bytes, gout_codes, gout_plane) for h in range(2)]
 
         def column(name, source, factor):
             col = tile(name, [P, 1])
@@ -120,17 +117,19 @@ def tile_attend_gppagetimessigmoid_kernel(tc, query, keys_words, keys_scales, th
 
         th_bias = column("th_bias", th_col, -0.5)
         neg_k = column("neg_k", sharp_col, -1.0 / PAGE)
-        neg_half_k = column("neg_half_k", sharp_col, -0.5 / PAGE)
+        half_k = column("half_k", sharp_col, 0.5 / PAGE)
         pen_k = column("pen_k", sharp_col, PENALTY / PAGE)
         neg_pen_k = column("neg_pen_k", sharp_col, -PENALTY / PAGE)
 
         gate = tile("gate", [P, I], F32, "gout_raw")
-        nc.scalar.activation(gate[:], score[:], ACT.Tanh, bias=th_bias[:], scale=0.5)
+        for h in range(2):
+            nc.scalar.activation(gate[:, halves[h]], score[h][:], ACT.Tanh, bias=th_bias[:], scale=0.5)
         gate_sq = tile("gate_sq", [P, I])
-        nc.scalar.activation(gate_sq[:], gate[:], ACT.Square)
+        nc.scalar.activation(gate_sq[:], gate[:], ACT.Square, scale=0.5)
 
         score_sum = tile("score_sum", [P, G], F32, "vals_plane")
-        nc.vector.tensor_reduce(score_sum[:], pages(score[:]), AXIS_X, add)
+        for h in range(2):
+            nc.vector.tensor_reduce(score_sum[:, half_pages[h]], pages(score[h][:]), AXIS_X, add)
         neg_s = tile("neg_s", [P, G])
         neg_top = tile("neg_top", [P, 1])
         nc.vector.tensor_scalar(neg_s[:], score_sum[:], neg_k[:], None, mult, ALU.min, accum_out=neg_top[:])
@@ -141,70 +140,77 @@ def tile_attend_gppagetimessigmoid_kernel(tc, query, keys_words, keys_scales, th
         nc.vector.reciprocal(z_inv[:], z[:])
         r = tile("r", [P, G])
         nc.vector.tensor_scalar(r[:], p[:], z_inv[:], None, mult)
-        neg_r = tile("neg_r", [P, G])
-        nc.vector.tensor_scalar(neg_r[:], p[:], z_inv[:], -1.0, mult, mult)
-        value_product(1, "p")
-        slope = tile("slope", [P, I])
+        neg_quarter_p = tile("neg_quarter_p", [P, G])
+        nc.scalar.mul(neg_quarter_p[:], p[:], -0.25)
+
+        neg_slope = tile("neg_slope", [P, I])
         for g in range(G):
-            cols = slice(g * PAGE, (g + 1) * PAGE)
-            nc.scalar.activation(slope[:, cols], gate_sq[:, cols], ACT.Identity, bias=neg_r[:, g : g + 1], scale=r[:, g : g + 1])
+            nc.scalar.activation(neg_slope[:, page_cols(g)], gate_sq[:, page_cols(g)], ACT.Identity,
+                                 bias=neg_quarter_p[:, g : g + 1], scale=p[:, g : g + 1])
 
-        for h in range(2):
-            cols = slice(h * HALF, (h + 1) * HALF)
+        drr2 = tile("drr2", [P, I])
+        for h, cols in enumerate(halves):
             nc.vector.scalar_tensor_tensor(drr2[:, cols], gate[:, cols], 1.0, c0[h][:], add, mult)
-        for h in range(2):
-            cols = slice(h * HALF, (h + 1) * HALF)
-            nc.vector.scalar_tensor_tensor(w[:, cols], c0[h][:], -0.25, slope[:, cols], mult, mult)
-        w_sq = tile("w_sq", [P, I])
-        nc.scalar.activation(w_sq[:], w[:], ACT.Square)
-
         dr2 = tile("dr2", [P, G])
         nc.vector.tensor_reduce(dr2[:], pages(drr2[:]), AXIS_X, add)
-        w_sum = tile("w_sum", [P, G])
-        nc.vector.tensor_reduce(w_sum[:], pages(w[:]), AXIS_X, add)
-        neg_krd = tile("neg_krd", [P, G])
-        neg_km = tile("neg_km", [P, 1])
-        nc.vector.scalar_tensor_tensor(neg_krd[:], dr2[:], neg_half_k[:], r[:], mult, mult, accum_out=neg_km[:])
+        krd = tile("krd", [P, G])
+        km = tile("km", [P, 1])
+        nc.vector.scalar_tensor_tensor(krd[:], dr2[:], half_k[:], r[:], mult, mult, accum_out=km[:])
+        neg_e1 = tile("neg_e1", [P, G])
+        nc.vector.scalar_tensor_tensor(neg_e1[:], r[:], km[:], krd[:], mult, sub)
+
+        neg_w = tile("neg_w", [P, I])
+        w_sq = tile("w_sq", [P, I])
+        for h, cols in enumerate(halves):
+            nc.vector.scalar_tensor_tensor(neg_w[:, cols], c0[h][:], z_inv[:], neg_slope[:, cols], mult, mult)
+            nc.scalar.activation(w_sq[:, cols], neg_w[:, cols], ACT.Square)
+
+        neg_w_sum = tile("neg_w_sum", [P, G])
+        nc.vector.tensor_reduce(neg_w_sum[:], pages(neg_w[:]), AXIS_X, add)
+        neg_da_sum = tile("neg_da_sum", [P, G])
+        nc.vector.scalar_tensor_tensor(neg_da_sum[:], neg_e1[:], float(PAGE), neg_w_sum[:], mult, add)
+        neg_da = tile("neg_da", [P, I])
+        for g in range(G):
+            nc.scalar.activation(neg_da[:, page_cols(g)], neg_w[:, page_cols(g)], ACT.Identity, bias=neg_e1[:, g : g + 1])
+        def bend_half(h, tag):
+            half = tile("bend%d" % h, [P, HALF], F32, tag)
+            nc.vector.scalar_tensor_tensor(half[:], neg_da[:, halves[h]], -PENALTY, gate[:, halves[h]], mult, mult)
+            return half
+
+        bend = [bend_half(0, None)]
+        neg_r_hds = tile("neg_r_hds", [P, G])
+        neg_hds_mean = tile("neg_hds_mean", [P, 1])
+        nc.vector.scalar_tensor_tensor(neg_r_hds[:], neg_da_sum[:], pen_k[:], r[:], mult, mult, accum_out=neg_hds_mean[:])
         w_sq_sum = tile("w_sq_sum", [P, G])
         nc.vector.tensor_reduce(w_sq_sum[:], pages(w_sq[:]), AXIS_X, add)
-        e1 = tile("e1", [P, G])
-        nc.vector.scalar_tensor_tensor(e1[:], r[:], neg_km[:], neg_krd[:], mult, sub)
-        da_sum = tile("da_sum", [P, G])
-        nc.vector.scalar_tensor_tensor(da_sum[:], e1[:], float(PAGE), w_sum[:], mult, add)
-        da = tile("da", [P, I])
-        for g in range(G):
-            cols = slice(g * PAGE, (g + 1) * PAGE)
-            nc.scalar.activation(da[:, cols], w[:, cols], ACT.Identity, bias=e1[:, g : g + 1])
-        r_hds = tile("r_hds", [P, G])
-        hds_mean = tile("hds_mean", [P, 1])
-        nc.vector.scalar_tensor_tensor(r_hds[:], da_sum[:], pen_k[:], r[:], mult, mult, accum_out=hds_mean[:])
-        hds_c = tile("hds_c", [P, G])
-        nc.vector.tensor_scalar(hds_c[:], da_sum[:], pen_k[:], hds_mean[:], mult, sub)
-        neg_j = tile("neg_j", [P, G])
-        nc.vector.scalar_tensor_tensor(neg_j[:], w_sum[:], neg_pen_k[:], hds_c[:], mult, sub)
+        neg_hds_c = tile("neg_hds_c", [P, G])
+        nc.vector.tensor_scalar(neg_hds_c[:], neg_da_sum[:], pen_k[:], neg_hds_mean[:], mult, sub)
+        bend.append(bend_half(1, None))
+        j = tile("j", [P, G])
+        nc.vector.scalar_tensor_tensor(j[:], neg_w_sum[:], neg_pen_k[:], neg_hds_c[:], mult, sub)
         neg_l = tile("neg_l", [P, G])
-        nc.vector.tensor_tensor(neg_l[:], neg_j[:], e1[:], mult)
+        nc.vector.tensor_tensor(neg_l[:], j[:], neg_e1[:], mult)
         neg_tau = tile("neg_tau", [P, G])
         neg_tau_sum = tile("neg_tau_sum", [P, 1])
         nc.vector.scalar_tensor_tensor(neg_tau[:], w_sq_sum[:], neg_pen_k[:], neg_l[:], mult, add, accum_out=neg_tau_sum[:])
         e52 = tile("e52", [P, G])
         nc.vector.scalar_tensor_tensor(e52[:], r[:], neg_tau_sum[:], neg_tau[:], mult, sub)
-        based = tile("based", [P, I])
-        for g in range(G):
-            cols = slice(g * PAGE, (g + 1) * PAGE)
-            nc.scalar.activation(based[:, cols], base_sb[:, cols], ACT.Identity, bias=e52[:, g : g + 1])
-        bend = tile("bend", [P, I])
+
         factor = tile("factor", [P, I])
-        slot_term = tile("slot_term", [P, I])
+        based = tile("based", [P, I])
         result = tile("result", [P, I])
-        halves = [slice(h * HALF, (h + 1) * HALF) for h in range(2)]
-        for cols in halves:
-            nc.vector.scalar_tensor_tensor(bend[:, cols], da[:, cols], -PENALTY, gate[:, cols], mult, mult)
-        for h, cols in enumerate(halves):
-            nc.vector.tensor_tensor(pages(factor[:, cols]), pages(bend[:, cols]),
-                                    spread(hds_c[:, h * G // 2 : (h + 1) * G // 2]), add)
-        for cols in halves:
-            nc.vector.tensor_tensor(slot_term[:, cols], factor[:, cols], w[:, cols], mult)
-        for cols in halves:
-            nc.vector.tensor_tensor(result[:, cols], slot_term[:, cols], based[:, cols], add)
-            nc.sync.dma_start(out[:, cols], result[:, cols])
+        first, second = halves
+        for g in range(G):
+            nc.scalar.activation(factor[:, page_cols(g)], bend[g // (G // 2)][:, page_cols(g % (G // 2))], ACT.Identity,
+                                 bias=neg_hds_c[:, g : g + 1])
+        slot_first = tile("slot_first", [P, HALF])
+        nc.vector.tensor_tensor(slot_first[:], factor[:, first], neg_w[:, first], mult)
+        nc.vector.tensor_tensor(based[:, first], slot_first[:], base_sb[:, first], add)
+        for g in range(G // 2, G):
+            nc.scalar.activation(based[:, page_cols(g)], base_sb[:, page_cols(g)], ACT.Identity, bias=e52[:, g : g + 1])
+        slot_second = tile("slot_second", [P, HALF], F32, "neg_tau")
+        nc.vector.tensor_tensor(slot_second[:], factor[:, second], neg_w[:, second], mult)
+        nc.vector.tensor_tensor(pages(result[:, first]), pages(based[:, first]), spread(e52[:, half_pages[0]]), add)
+        nc.sync.dma_start(out[:, first], result[:, first])
+        nc.vector.tensor_tensor(result[:, second], slot_second[:], based[:, second], add)
+        nc.sync.dma_start(out[:, second], result[:, second])

@@ -18,6 +18,9 @@ AXIS_X = mybir.AxisListType.X
 
 P = 128
 PACK = 4
+QUAD = 32
+QUAD_ROWS = 4
+LIST_ROWS = 16
 PAGE = I // G
 HALF = I // 2
 PENALTY = 32.0 * 2.0 * 32.0
@@ -32,8 +35,8 @@ def tile_attend_gppagetimessigmoid_kernel(tc, query, keys_words, keys_scales, th
         sb = ctx.enter_context(tc.tile_pool(name="sb", bufs=1))
         ps = ctx.enter_context(tc.psum_pool(name="ps", bufs=1))
 
-        def tile(name, shape, dtype=F32, tag=None):
-            return sb.tile(shape, dtype, name=name, tag=tag or name, align_bytes=64)
+        def tile(name, shape, dtype=F32, reuses=None):
+            return sb.tile(shape, dtype, name=name, tag=reuses or name, align_bytes=64)
 
         def pages(ap):
             return ap.rearrange("p (g j) -> p g j", j=PAGE)
@@ -41,17 +44,16 @@ def tile_attend_gppagetimessigmoid_kernel(tc, query, keys_words, keys_scales, th
         def spread(ap):
             return ap.unsqueeze(2).to_broadcast([P, ap.shape[1], PAGE])
 
-        def load_words(name, words, tag=None):
-            pool_words = tile(name, [P, T], I32, tag)
+        def load_words(name, words):
+            pool_words = tile(name, [P, T], I32)
             nc.sync.dma_start(pool_words[:], words[0].rearrange("p t r -> p (t r)").bitcast(I32))
             return pool_words
 
-        def load_scales(name, scales, zero_engine, queue):
+        def load_scales(name, scales):
             plane = tile(name, [P, T], U8)
-            zero_engine.memset(plane[:].bitcast(I32), 0)
-            for quad in range(4):
-                queue.dma_start(plane[32 * quad : 32 * quad + 4, :].bitcast(I32),
-                                scales[0, 4 * quad : 4 * quad + 4, :].bitcast(I32))
+            nc.vector.memset(plane[:].bitcast(I32), 0)
+            for row in range(QUAD_ROWS):
+                nc.sync.dma_start(plane[row:P:QUAD, :].bitcast(I32), scales[0, row : P // QUAD * QUAD_ROWS : QUAD_ROWS, :].bitcast(I32))
             return plane
 
         def load_rows(name, rows):
@@ -68,16 +70,16 @@ def tile_attend_gppagetimessigmoid_kernel(tc, query, keys_words, keys_scales, th
                                   in_=woven[:].rearrange("p q r -> p (q r)"))
             return codes, plane
 
-        offsets = sb.tile([P, I // 16], U16, name="offsets")
+        offsets = sb.tile([P, I // LIST_ROWS], U16, name="offsets")
         nc.sync.dma_start(offsets[:], offs)
         query_raw = load_rows("query_raw", query)
         sharp_col = tile("sharp_col", [P, 1])
         nc.sync.dma_start(sharp_col[:], sharp)
-        keys_plane = load_scales("keys_plane", keys_scales, nc.vector, nc.sync)
+        keys_plane = load_scales("keys_plane", keys_scales)
         keys_pool = load_words("keys_pool", keys_words)
         th_col = tile("th_col", [P, 1])
         nc.sync.dma_start(th_col[:], th)
-        vals_plane = load_scales("vals_plane", vals_scales, nc.vector, nc.sync)
+        vals_plane = load_scales("vals_plane", vals_scales)
         gout_raw = load_rows("gout_raw", gout)
         vals_pool = load_words("vals_pool", vals_words)
         base_sb = tile("base_sb", [P, I])
@@ -86,48 +88,48 @@ def tile_attend_gppagetimessigmoid_kernel(tc, query, keys_words, keys_scales, th
 
         halves = [slice(h * HALF, (h + 1) * HALF) for h in range(2)]
         half_pages = [slice(h * G // 2, (h + 1) * G // 2) for h in range(2)]
-        half_list = [offsets[:, h * HALF // 16 : (h + 1) * HALF // 16] for h in range(2)]
+        half_list = [offsets[:, h * HALF // LIST_ROWS : (h + 1) * HALF // LIST_ROWS] for h in range(2)]
 
         def page_cols(g):
             return slice(g * PAGE, (g + 1) * PAGE)
 
-        def product(name, h, pool_words, picked_bytes, codes, plane, tag=None):
-            picked = tile("%s_codes%d" % (name, h), [P, HALF], U32, tag)
+        def product(name, h, pool_words, picked_plane, row_codes, row_plane, reuses=None):
+            picked = tile("%s_codes%d" % (name, h), [P, HALF], U32, reuses)
             nc.vector.tensor_copy(picked[:], pool_words[:].bitcast(U32).indirect(half_list[h]))
             bank = ps.tile([P, HALF], F32, name="%s_bank%d" % (name, h))
-            nc.tensor.matmul_mx(out=bank[:], lhsT=codes[:].bitcast(FP8X4), lhsT_scale=plane[:],
-                                rhs=picked[:].bitcast(FP8X4), rhs_scale=picked_bytes[:, halves[h]],
+            nc.tensor.matmul_mx(out=bank[:], lhsT=row_codes[:].bitcast(FP8X4), lhsT_scale=row_plane[:],
+                                rhs=picked[:].bitcast(FP8X4), rhs_scale=picked_plane[:, halves[h]],
                                 start=True, stop=True)
             return bank
 
-        keys_bytes = tile("keys_bytes", [P, I], U8)
-        nc.vector.tensor_copy(keys_bytes[:], keys_plane[:].indirect(offsets[:]))
-        score = [product("keys", 0, keys_pool, keys_bytes, query_codes, query_plane, "keys_plane"),
-                 product("keys", 1, keys_pool, keys_bytes, query_codes, query_plane)]
+        keys_picked_plane = tile("keys_bytes", [P, I], U8)
+        nc.vector.tensor_copy(keys_picked_plane[:], keys_plane[:].indirect(offsets[:]))
+        score = [product("keys", 0, keys_pool, keys_picked_plane, query_codes, query_plane, reuses="keys_plane"),
+                 product("keys", 1, keys_pool, keys_picked_plane, query_codes, query_plane)]
 
         gout_codes, gout_plane = quantise("gout", gout_raw)
-        vals_bytes = tile("vals_bytes", [P, I], U8)
-        nc.vector.tensor_copy(vals_bytes[:], vals_plane[:].indirect(offsets[:]))
-        c0 = [product("vals", h, vals_pool, vals_bytes, gout_codes, gout_plane) for h in range(2)]
+        vals_picked_plane = tile("vals_bytes", [P, I], U8)
+        nc.vector.tensor_copy(vals_picked_plane[:], vals_plane[:].indirect(offsets[:]))
+        c0 = [product("vals", h, vals_pool, vals_picked_plane, gout_codes, gout_plane) for h in range(2)]
 
-        def column(name, source, factor):
+        def column(name, source, times):
             col = tile(name, [P, 1])
-            nc.scalar.mul(col[:], source[:], factor)
+            nc.scalar.mul(col[:], source[:], times)
             return col
 
-        th_bias = column("th_bias", th_col, -0.5)
+        neg_half_th = column("th_bias", th_col, -0.5)
         neg_k = column("neg_k", sharp_col, -1.0 / PAGE)
         half_k = column("half_k", sharp_col, 0.5 / PAGE)
         pen_k = column("pen_k", sharp_col, PENALTY / PAGE)
         neg_pen_k = column("neg_pen_k", sharp_col, -PENALTY / PAGE)
 
-        gate = tile("gate", [P, I], F32, "gout_raw")
+        gate = tile("gate", [P, I], reuses="gout_raw")
         for h in range(2):
-            nc.scalar.activation(gate[:, halves[h]], score[h][:], ACT.Tanh, bias=th_bias[:], scale=0.5)
-        gate_sq = tile("gate_sq", [P, I])
-        nc.scalar.activation(gate_sq[:], gate[:], ACT.Square, scale=0.5)
+            nc.scalar.activation(gate[:, halves[h]], score[h][:], ACT.Tanh, bias=neg_half_th[:], scale=0.5)
+        half_gate_sq = tile("gate_sq", [P, I])
+        nc.scalar.activation(half_gate_sq[:], gate[:], ACT.Square, scale=0.5)
 
-        score_sum = tile("score_sum", [P, G], F32, "vals_plane")
+        score_sum = tile("score_sum", [P, G], reuses="vals_plane")
         for h in range(2):
             nc.vector.tensor_reduce(score_sum[:, half_pages[h]], pages(score[h][:]), AXIS_X, add)
         neg_s = tile("neg_s", [P, G])
@@ -145,19 +147,19 @@ def tile_attend_gppagetimessigmoid_kernel(tc, query, keys_words, keys_scales, th
 
         neg_slope = tile("neg_slope", [P, I])
         for g in range(G):
-            nc.scalar.activation(neg_slope[:, page_cols(g)], gate_sq[:, page_cols(g)], ACT.Identity,
+            nc.scalar.activation(neg_slope[:, page_cols(g)], half_gate_sq[:, page_cols(g)], ACT.Identity,
                                  bias=neg_quarter_p[:, g : g + 1], scale=p[:, g : g + 1])
 
-        drr2 = tile("drr2", [P, I])
+        twice_drr = tile("drr2", [P, I])
         for h, cols in enumerate(halves):
-            nc.vector.scalar_tensor_tensor(drr2[:, cols], gate[:, cols], 1.0, c0[h][:], add, mult)
-        dr2 = tile("dr2", [P, G])
-        nc.vector.tensor_reduce(dr2[:], pages(drr2[:]), AXIS_X, add)
-        krd = tile("krd", [P, G])
-        km = tile("km", [P, 1])
-        nc.vector.scalar_tensor_tensor(krd[:], dr2[:], half_k[:], r[:], mult, mult, accum_out=km[:])
+            nc.vector.scalar_tensor_tensor(twice_drr[:, cols], gate[:, cols], 1.0, c0[h][:], add, mult)
+        twice_dr = tile("dr2", [P, G])
+        nc.vector.tensor_reduce(twice_dr[:], pages(twice_drr[:]), AXIS_X, add)
+        k_r_dr = tile("krd", [P, G])
+        k_r_dr_total = tile("km", [P, 1])
+        nc.vector.scalar_tensor_tensor(k_r_dr[:], twice_dr[:], half_k[:], r[:], mult, mult, accum_out=k_r_dr_total[:])
         neg_e1 = tile("neg_e1", [P, G])
-        nc.vector.scalar_tensor_tensor(neg_e1[:], r[:], km[:], krd[:], mult, sub)
+        nc.vector.scalar_tensor_tensor(neg_e1[:], r[:], k_r_dr_total[:], k_r_dr[:], mult, sub)
 
         neg_w = tile("neg_w", [P, I])
         w_sq = tile("w_sq", [P, I])
@@ -172,12 +174,13 @@ def tile_attend_gppagetimessigmoid_kernel(tc, query, keys_words, keys_scales, th
         neg_da = tile("neg_da", [P, I])
         for g in range(G):
             nc.scalar.activation(neg_da[:, page_cols(g)], neg_w[:, page_cols(g)], ACT.Identity, bias=neg_e1[:, g : g + 1])
-        def bend_half(h, tag):
-            half = tile("bend%d" % h, [P, HALF], F32, tag)
+
+        def bend_half(h):
+            half = tile("bend%d" % h, [P, HALF])
             nc.vector.scalar_tensor_tensor(half[:], neg_da[:, halves[h]], -PENALTY, gate[:, halves[h]], mult, mult)
             return half
 
-        bend = [bend_half(0, None)]
+        bend = [bend_half(0)]
         neg_r_hds = tile("neg_r_hds", [P, G])
         neg_hds_mean = tile("neg_hds_mean", [P, 1])
         nc.vector.scalar_tensor_tensor(neg_r_hds[:], neg_da_sum[:], pen_k[:], r[:], mult, mult, accum_out=neg_hds_mean[:])
@@ -185,32 +188,34 @@ def tile_attend_gppagetimessigmoid_kernel(tc, query, keys_words, keys_scales, th
         nc.vector.tensor_reduce(w_sq_sum[:], pages(w_sq[:]), AXIS_X, add)
         neg_hds_c = tile("neg_hds_c", [P, G])
         nc.vector.tensor_scalar(neg_hds_c[:], neg_da_sum[:], pen_k[:], neg_hds_mean[:], mult, sub)
-        bend.append(bend_half(1, None))
-        j = tile("j", [P, G])
-        nc.vector.scalar_tensor_tensor(j[:], neg_w_sum[:], neg_pen_k[:], neg_hds_c[:], mult, sub)
-        neg_l = tile("neg_l", [P, G])
-        nc.vector.tensor_tensor(neg_l[:], j[:], neg_e1[:], mult)
+        bend.append(bend_half(1))
+        e1_weight = tile("j", [P, G])
+        nc.vector.scalar_tensor_tensor(e1_weight[:], neg_w_sum[:], neg_pen_k[:], neg_hds_c[:], mult, sub)
+        neg_e1_term = tile("neg_l", [P, G])
+        nc.vector.tensor_tensor(neg_e1_term[:], e1_weight[:], neg_e1[:], mult)
         neg_tau = tile("neg_tau", [P, G])
-        neg_tau_sum = tile("neg_tau_sum", [P, 1])
-        nc.vector.scalar_tensor_tensor(neg_tau[:], w_sq_sum[:], neg_pen_k[:], neg_l[:], mult, add, accum_out=neg_tau_sum[:])
+        neg_tau_total = tile("neg_tau_sum", [P, 1])
+        nc.vector.scalar_tensor_tensor(neg_tau[:], w_sq_sum[:], neg_pen_k[:], neg_e1_term[:], mult, add,
+                                       accum_out=neg_tau_total[:])
         e52 = tile("e52", [P, G])
-        nc.vector.scalar_tensor_tensor(e52[:], r[:], neg_tau_sum[:], neg_tau[:], mult, sub)
+        nc.vector.scalar_tensor_tensor(e52[:], r[:], neg_tau_total[:], neg_tau[:], mult, sub)
 
-        factor = tile("factor", [P, I])
+        neg_factor = tile("factor", [P, I])
         based = tile("based", [P, I])
         result = tile("result", [P, I])
         first, second = halves
         for g in range(G):
-            nc.scalar.activation(factor[:, page_cols(g)], bend[g // (G // 2)][:, page_cols(g % (G // 2))], ACT.Identity,
+            h, g_in_half = divmod(g, G // 2)
+            nc.scalar.activation(neg_factor[:, page_cols(g)], bend[h][:, page_cols(g_in_half)], ACT.Identity,
                                  bias=neg_hds_c[:, g : g + 1])
-        slot_first = tile("slot_first", [P, HALF])
-        nc.vector.tensor_tensor(slot_first[:], factor[:, first], neg_w[:, first], mult)
-        nc.vector.tensor_tensor(based[:, first], slot_first[:], base_sb[:, first], add)
+        w_factor_first = tile("slot_first", [P, HALF])
+        nc.vector.tensor_tensor(w_factor_first[:], neg_factor[:, first], neg_w[:, first], mult)
+        nc.vector.tensor_tensor(based[:, first], w_factor_first[:], base_sb[:, first], add)
         for g in range(G // 2, G):
             nc.scalar.activation(based[:, page_cols(g)], base_sb[:, page_cols(g)], ACT.Identity, bias=e52[:, g : g + 1])
-        slot_second = tile("slot_second", [P, HALF], F32, "neg_tau")
-        nc.vector.tensor_tensor(slot_second[:], factor[:, second], neg_w[:, second], mult)
+        w_factor_second = tile("slot_second", [P, HALF], reuses="neg_tau")
+        nc.vector.tensor_tensor(w_factor_second[:], neg_factor[:, second], neg_w[:, second], mult)
         nc.vector.tensor_tensor(pages(result[:, first]), pages(based[:, first]), spread(e52[:, half_pages[0]]), add)
         nc.sync.dma_start(out[:, first], result[:, first])
-        nc.vector.tensor_tensor(result[:, second], slot_second[:], based[:, second], add)
+        nc.vector.tensor_tensor(result[:, second], w_factor_second[:], based[:, second], add)
         nc.sync.dma_start(out[:, second], result[:, second])

from contextlib import ExitStack

import concourse.mybir as mybir

D, E, T, I, Q, G = 512, 512, 2048, 512, 128, 32
FLOPS = 2 * D * Q * I + 2 * E * Q * I

F32 = mybir.dt.float32
BF16 = mybir.dt.bfloat16
I32 = mybir.dt.int32
U32 = mybir.dt.uint32
U16 = mybir.dt.uint16
U8 = mybir.dt.uint8
FP8X4 = mybir.dt.float8_e4m3fn_x4
ALU = mybir.AluOpType
ACT = mybir.ActivationFunctionType
AXIS_X = mybir.AxisListType.X

P = 128
PACK = 4
QUAD = 32
QUAD_ROWS = 4
LIST_ROWS = 16
PAGE = I // G
HALF = I // 2
PENALTY = 32.0 * 2.0 * 32.0


def tile_attend_gppagetimessigmoid_kernel(tc, query, keys_words, keys_scales, th, sharp, gout,
                                           vals_words, vals_scales, base, offs, out):
    nc = tc.nc
    mult, add, sub = ALU.mult, ALU.add, ALU.subtract

    with ExitStack() as ctx:
        sb = ctx.enter_context(tc.tile_pool(name="sb", bufs=1))
        ps = ctx.enter_context(tc.psum_pool(name="ps", bufs=1))

        def tile(name, shape, dtype=F32, reuses=None):
            return sb.tile(shape, dtype, name=name, tag=reuses or name, align_bytes=64)

        def pages(ap):
            return ap.rearrange("p (g j) -> p g j", j=PAGE)

        def spread(ap):
            return ap.unsqueeze(2).to_broadcast([P, ap.shape[1], PAGE])

        def load_words(name, words):
            pool_words = tile(name, [P, T], I32)
            nc.sync.dma_start(pool_words[:], words[0].rearrange("p t r -> p (t r)").bitcast(I32))
            return pool_words

        def load_scales(name, scales):
            plane = tile(name, [P, T], U8)
            nc.vector.memset(plane[:].bitcast(I32), 0)
            for row in range(QUAD_ROWS):
                nc.sync.dma_start(plane[row:P:QUAD, :].bitcast(I32), scales[0, row : P // QUAD * QUAD_ROWS : QUAD_ROWS, :].bitcast(I32))
            return plane

        def load_rows(name, rows):
            raw = tile(name, [P, PACK, Q])
            nc.sync.dma_start(raw[:], rows.rearrange("(p r) q -> p r q", r=PACK))
            return raw

        def quantise(name, raw):
            woven = tile(name + "_woven", [P, Q, PACK], BF16)
            nc.scalar.copy(woven[:], raw[:].rearrange("p r q -> p q r"))
            codes = tile(name + "_codes", [P, Q], U32)
            plane = tile(name + "_plane", [P, Q], U8)
            nc.vector.quantize_mx(out=codes[:].bitcast(FP8X4), scales=plane[:],
                                  in_=woven[:].rearrange("p q r -> p (q r)"))
            return codes, plane

        offsets = sb.tile([P, I // LIST_ROWS], U16, name="offsets")
        nc.sync.dma_start(offsets[:], offs)
        query_raw = load_rows("query_raw", query)
        sharp_col = tile("sharp_col", [P, 1])
        nc.sync.dma_start(sharp_col[:], sharp)
        keys_plane = load_scales("keys_plane", keys_scales)
        keys_pool = load_words("keys_pool", keys_words)
        th_col = tile("th_col", [P, 1])
        nc.sync.dma_start(th_col[:], th)
        vals_plane = load_scales("vals_plane", vals_scales)
        gout_raw = load_rows("gout_raw", gout)
        vals_pool = load_words("vals_pool", vals_words)
        base_sb = tile("base_sb", [P, I])
        nc.sync.dma_start(base_sb[:], base)
        query_codes, query_plane = quantise("query", query_raw)

        halves = [slice(h * HALF, (h + 1) * HALF) for h in range(2)]
        half_pages = [slice(h * G // 2, (h + 1) * G // 2) for h in range(2)]
        half_list = [offsets[:, h * HALF // LIST_ROWS : (h + 1) * HALF // LIST_ROWS] for h in range(2)]

        def page_cols(g):
            return slice(g * PAGE, (g + 1) * PAGE)

        def product(name, h, pool_words, picked_plane, row_codes, row_plane, reuses=None):
            picked = tile("%s_codes%d" % (name, h), [P, HALF], U32, reuses)
            nc.vector.tensor_copy(picked[:], pool_words[:].bitcast(U32).indirect(half_list[h]))
            bank = ps.tile([P, HALF], F32, name="%s_bank%d" % (name, h))
            nc.tensor.matmul_mx(out=bank[:], lhsT=row_codes[:].bitcast(FP8X4), lhsT_scale=row_plane[:],
                                rhs=picked[:].bitcast(FP8X4), rhs_scale=picked_plane[:, halves[h]],
                                start=True, stop=True)
            return bank

        keys_picked_plane = tile("keys_bytes", [P, I], U8)
        nc.vector.tensor_copy(keys_picked_plane[:], keys_plane[:].indirect(offsets[:]))
        score = [product("keys", 0, keys_pool, keys_picked_plane, query_codes, query_plane, reuses="keys_plane"),
                 product("keys", 1, keys_pool, keys_picked_plane, query_codes, query_plane)]

        gout_codes, gout_plane = quantise("gout", gout_raw)
        vals_picked_plane = tile("vals_bytes", [P, I], U8)
        nc.vector.tensor_copy(vals_picked_plane[:], vals_plane[:].indirect(offsets[:]))
        c0 = [product("vals", h, vals_pool, vals_picked_plane, gout_codes, gout_plane) for h in range(2)]

        def column(name, source, times):
            col = tile(name, [P, 1])
            nc.scalar.mul(col[:], source[:], times)
            return col

        neg_half_th = column("th_bias", th_col, -0.5)
        neg_k = column("neg_k", sharp_col, -1.0 / PAGE)
        half_k = column("half_k", sharp_col, 0.5 / PAGE)
        pen_k = column("pen_k", sharp_col, PENALTY / PAGE)
        neg_pen_k = column("neg_pen_k", sharp_col, -PENALTY / PAGE)

        gate = tile("gate", [P, I], reuses="gout_raw")
        for h in range(2):
            nc.scalar.activation(gate[:, halves[h]], score[h][:], ACT.Tanh, bias=neg_half_th[:], scale=0.5)
        half_gate_sq = tile("gate_sq", [P, I])
        nc.scalar.activation(half_gate_sq[:], gate[:], ACT.Square, scale=0.5)

        score_sum = tile("score_sum", [P, G], reuses="vals_plane")
        for h in range(2):
            nc.vector.tensor_reduce(score_sum[:, half_pages[h]], pages(score[h][:]), AXIS_X, add)
        neg_s = tile("neg_s", [P, G])
        neg_top = tile("neg_top", [P, 1])
        nc.vector.tensor_scalar(neg_s[:], score_sum[:], neg_k[:], None, mult, ALU.min, accum_out=neg_top[:])
        p = tile("p", [P, G])
        z = tile("z", [P, 1])
        nc.scalar.activation(p[:], neg_s[:], ACT.Exp, bias=neg_top[:], scale=-1.0, accum_out=z[:])
        z_inv = tile("z_inv", [P, 1])
        nc.vector.reciprocal(z_inv[:], z[:])
        r = tile("r", [P, G])
        nc.vector.tensor_scalar(r[:], p[:], z_inv[:], None, mult)
        neg_quarter_p = tile("neg_quarter_p", [P, G])
        nc.scalar.mul(neg_quarter_p[:], p[:], -0.25)

        neg_slope = tile("neg_slope", [P, I])
        for g in range(G):
            nc.scalar.activation(neg_slope[:, page_cols(g)], half_gate_sq[:, page_cols(g)], ACT.Identity,
                                 bias=neg_quarter_p[:, g : g + 1], scale=p[:, g : g + 1])

        twice_drr = tile("drr2", [P, I])
        for h, cols in enumerate(halves):
            nc.vector.scalar_tensor_tensor(twice_drr[:, cols], gate[:, cols], 1.0, c0[h][:], add, mult)
        twice_dr = tile("dr2", [P, G])
        nc.vector.tensor_reduce(twice_dr[:], pages(twice_drr[:]), AXIS_X, add)
        k_r_dr = tile("krd", [P, G])
        k_r_dr_total = tile("km", [P, 1])
        nc.vector.scalar_tensor_tensor(k_r_dr[:], twice_dr[:], half_k[:], r[:], mult, mult, accum_out=k_r_dr_total[:])
        neg_e1 = tile("neg_e1", [P, G])
        nc.vector.scalar_tensor_tensor(neg_e1[:], r[:], k_r_dr_total[:], k_r_dr[:], mult, sub)

        neg_w = tile("neg_w", [P, I])
        w_sq = tile("w_sq", [P, I])
        for h, cols in enumerate(halves):
            nc.vector.scalar_tensor_tensor(neg_w[:, cols], c0[h][:], z_inv[:], neg_slope[:, cols], mult, mult)
            nc.scalar.activation(w_sq[:, cols], neg_w[:, cols], ACT.Square)

        neg_w_sum = tile("neg_w_sum", [P, G])
        nc.vector.tensor_reduce(neg_w_sum[:], pages(neg_w[:]), AXIS_X, add)
        neg_da_sum = tile("neg_da_sum", [P, G])
        nc.vector.scalar_tensor_tensor(neg_da_sum[:], neg_e1[:], float(PAGE), neg_w_sum[:], mult, add)
        neg_da = tile("neg_da", [P, I])
        for g in range(G):
            nc.scalar.activation(neg_da[:, page_cols(g)], neg_w[:, page_cols(g)], ACT.Identity, bias=neg_e1[:, g : g + 1])

        def bend_half(h):
            half = tile("bend%d" % h, [P, HALF])
            nc.vector.scalar_tensor_tensor(half[:], neg_da[:, halves[h]], -PENALTY, gate[:, halves[h]], mult, mult)
            return half

        bend = [bend_half(0)]
        neg_r_hds = tile("neg_r_hds", [P, G])
        neg_hds_mean = tile("neg_hds_mean", [P, 1])
        nc.vector.scalar_tensor_tensor(neg_r_hds[:], neg_da_sum[:], pen_k[:], r[:], mult, mult, accum_out=neg_hds_mean[:])
        w_sq_sum = tile("w_sq_sum", [P, G])
        nc.vector.tensor_reduce(w_sq_sum[:], pages(w_sq[:]), AXIS_X, add)
        neg_hds_c = tile("neg_hds_c", [P, G])
        nc.vector.tensor_scalar(neg_hds_c[:], neg_da_sum[:], pen_k[:], neg_hds_mean[:], mult, sub)
        bend.append(bend_half(1))
        e1_weight = tile("j", [P, G])
        nc.vector.scalar_tensor_tensor(e1_weight[:], neg_w_sum[:], neg_pen_k[:], neg_hds_c[:], mult, sub)
        neg_e1_term = tile("neg_l", [P, G])
        nc.vector.tensor_tensor(neg_e1_term[:], e1_weight[:], neg_e1[:], mult)
        neg_tau = tile("neg_tau", [P, G])
        neg_tau_total = tile("neg_tau_sum", [P, 1])
        nc.vector.scalar_tensor_tensor(neg_tau[:], w_sq_sum[:], neg_pen_k[:], neg_e1_term[:], mult, add,
                                       accum_out=neg_tau_total[:])
        e52 = tile("e52", [P, G])
        nc.vector.scalar_tensor_tensor(e52[:], r[:], neg_tau_total[:], neg_tau[:], mult, sub)

        neg_factor = tile("factor", [P, I])
        based = tile("based", [P, I])
        result = tile("result", [P, I])
        first, second = halves
        for g in range(G):
            h, g_in_half = divmod(g, G // 2)
            nc.scalar.activation(neg_factor[:, page_cols(g)], bend[h][:, page_cols(g_in_half)], ACT.Identity,
                                 bias=neg_hds_c[:, g : g + 1])
        w_factor_first = tile("slot_first", [P, HALF])
        nc.vector.tensor_tensor(w_factor_first[:], neg_factor[:, first], neg_w[:, first], mult)
        nc.vector.tensor_tensor(based[:, first], w_factor_first[:], base_sb[:, first], add)
        for g in range(G // 2, G):
            nc.scalar.activation(based[:, page_cols(g)], base_sb[:, page_cols(g)], ACT.Identity, bias=e52[:, g : g + 1])
        w_factor_second = tile("slot_second", [P, HALF], reuses="neg_tau")
        nc.vector.tensor_tensor(w_factor_second[:], neg_factor[:, second], neg_w[:, second], mult)
        nc.vector.tensor_tensor(pages(result[:, first]), pages(based[:, first]), spread(e52[:, half_pages[0]]), add)
        nc.sync.dma_start(out[:, first], result[:, first])
        nc.vector.tensor_tensor(result[:, second], w_factor_second[:], based[:, second], add)
        nc.sync.dma_start(out[:, second], result[:, second])
